import numpy as np, ml_dtypes
CORES = [24,48,72,152,176,200]
N = 6
TK = 512
def setup_inputs(rng):
    x = rng.standard_normal((N, 128, TK), dtype=np.float32).astype(ml_dtypes.bfloat16); w1 = (rng.standard_normal((N, 128, 128), dtype=np.float32) / 8).astype(ml_dtypes.bfloat16)
    wa = np.concatenate(list(w1.astype(np.float64)), axis=1)
    for r in range(N):
        while True:
            near = (np.abs(wa.T @ x[r].astype(np.float64)) < 2e-4).any(axis=0)
            if not near.any(): break
            x[r][:, near] = rng.standard_normal((128, int(near.sum())), dtype=np.float32).astype(ml_dtypes.bfloat16)
    return {"x": x, "dy": rng.standard_normal((N, 128, TK), dtype=np.float32).astype(ml_dtypes.bfloat16), "w1": w1, "w2t": (rng.standard_normal((N, 128, 128), dtype=np.float32) / 8).astype(ml_dtypes.bfloat16)}
def setup_inputs_big(rng):
    d = setup_inputs(rng)
    for k in ("x", "dy", "w1", "w2t"): d[k] = (d[k].astype(np.float32) * 1024.0).astype(d[k].dtype)
    return d
def setup_inputs_small(rng):
    d = setup_inputs(rng)
    for k in ("x", "dy", "w1", "w2t"): d[k] = (d[k].astype(np.float32) * (1 / 1024.0)).astype(d[k].dtype)
    return d
def setup_inputs_apart(rng):
    d = setup_inputs(rng)
    f = (10.0 ** rng.permutation(np.linspace(-1.5, 1.5, N))).astype(np.float32).reshape(N, 1, 1)
    for k in ("x", "dy", "w1", "w2t"): d[k] = (d[k].astype(np.float32) * f).astype(d[k].dtype)
    return d
def reference(x, dy, w1, w2t):
    X, DY, W1, W2T = x.astype(np.float64), dy.astype(np.float64), w1.astype(np.float64), w2t.astype(np.float64)
    dx = np.zeros((N, 128, TK))
    for r in range(N):
        for j in range(N):
            dx[r] += W1[j] @ ((W1[j].T @ X[r] > 0) * (W2T[j].T @ DY[r]))
    return {"dx": dx.astype(ml_dtypes.bfloat16)}

@@ -1,0 +1,189 @@
+from concourse.mybir import AluOpType, ActivationFunctionType
+
+SIM_CORES = 256
+NR = 6
+D = 128
+TK = 512
+HF = 256
+WB = 2 * D
+E_ON = 8
+E_OFF = 8
+
+SCRATCH = {
+    "wall": ("sbuf", [128, NR * WB], "bfloat16"),
+    "xs": ("sbuf", [128, TK], "bfloat16"),
+    "dys": ("sbuf", [128, TK], "bfloat16"),
+    "ident": ("sbuf", [128, D], "bfloat16"),
+    "w1t": ("sbuf", [128, NR * D], "bfloat16"),
+    "msk": ("sbuf", [128, 2 * HF], "bfloat16"),
+    "gbuf": ("sbuf", [128, 2 * NR * HF], "bfloat16"),
+    "outb": ("sbuf", [128, TK], "bfloat16"),
+    "z0": ("psum", [128, 512], "float32"), "z1": ("psum", [128, 512], "float32"),
+    "u0": ("psum", [128, 512], "float32"), "u1": ("psum", [128, 512], "float32"),
+    "acc0": ("psum", [128, 512], "float32"), "acc1": ("psum", [128, 512], "float32"),
+    "pt": ("psum", [128, 1024], "bfloat16"),
+}
+SEMAPHORES = (["wl", "xl", "dl", "one", "idr", "sent", "zs0", "zs1", "us0", "us1", "ms0", "ms1", "gs0", "gs1",
+               "tp", "tc", "dd0", "dd1", "ev0", "ev1", "st0", "st1"] + ["arr%d" % j for j in range(NR)])
+
+
+def _take(mask, n):
+    out, got, e = 0, 0, 0
+    while got < n:
+        if (mask >> e) & 1:
+            out |= 1 << e
+            got += 1
+        e += 1
+        if e > 64:
+            raise ValueError("mask too small")
+    return out
+
+
+def _plan(cores, topo):
+    n = len(cores)
+    direct, relays, keys = [], [], [[] for _ in range(n)]
+    for i, c in enumerate(cores):
+        rot = sorted((k for k in range(n) if k != i), key=lambda k: (k - i) % n)
+        dr = [k for k in rot if topo.may_write(c, cores[k])]
+        cr = [k for k in rot if not topo.may_write(c, cores[k])]
+        direct.append(dr)
+        for p, k in enumerate(dr):
+            keys[k].append(((1, p, 0), i))
+        q = sorted(dr + [i]).index(i)
+        mine = [a for a in range(SIM_CORES) if a not in cores and topo.host(a) == topo.host(c) and topo.chip(a) == topo.chip(c)
+                and all(topo.may_write(a, cores[k]) for k in cr)]
+        dies = [topo.die(c)] + sorted(set(topo.die(a) for a in mine if topo.die(a) != topo.die(c)))
+        nrel = (len(cr) + 1) // 2
+        rl, used = [], []
+        for r in range(nrel):
+            die = dies[(r + q) % len(dies)]
+            a = [a for a in mine if topo.die(a) == die and a not in used][0]
+            used.append(a)
+            dst = cr[r::nrel]
+            rl.append((a, dst))
+            for p, k in enumerate(dst):
+                keys[k].append(((2, p, 0 if die == topo.die(c) else 1), i))
+        relays.append(rl)
+    order = []
+    for d in range(n):
+        order.append([(0, d)] + [(key[0], j) for key, j in sorted(keys[d])])
+    return direct, relays, order
+
+
+def _send(g, T, topo, src, dst, j, mask):
+    rid, pid = topo.addr(dst, src)
+    blk = T.wall[:, j * WB:(j + 1) * WB]
+    g.remote_dma(out_ap=blk, in_ap=blk, remote_sem=T.sem["arr%d" % j], local_sem=T.sem.sent,
+                 pid=pid, routing_id=rid, dma_engine_mask=mask)
+
+
+def rank_program(g, core, T, topo):
+    cores = list(T.cores)
+    direct, relays, order = _plan(cores, topo)
+    S = T.sem
+
+    for i in range(NR):
+        for a, dst in relays[i]:
+            if a == core:
+                g.wait_ge(S["arr%d" % i], E_ON)
+                for k in dst:
+                    _send(g, T, topo, core, cores[k], i, _take(topo.mask(core, cores[k]), E_OFF))
+                g.wait_ge(S.sent, E_OFF * len(dst))
+    me = T.rank_of(core)
+    if me is None:
+        return
+
+    w1 = lambda j: T.wall[:, j * WB:j * WB + D]
+    w2 = lambda j: T.wall[:, j * WB + D:(j + 1) * WB]
+    w1t = lambda j: T.w1t[:, j * D:(j + 1) * D]
+    Z, U, ACC = [T.z0, T.z1], [T.u0, T.u1], [T.acc0, T.acc1]
+    ZS, US, MS, GS, DD = [S.zs0, S.zs1], [S.us0, S.us1], [S.ms0, S.ms1], [S.gs0, S.gs1], [S.dd0, S.dd1]
+    seq = order[me]
+    nu = 2 * len(seq)
+
+    g.sync.dma_start(w1(me), T.w1[:]).then_inc(S.wl, 16)
+    g.scalar.dma_start(w2(me), T.w2t[:]).then_inc(S.wl, 16)
+    g.sync.dma_start(T.xs[:], T.x[:]).then_inc(S.xl, 16)
+    g.scalar.dma_start(T.dys[:], T.dy[:]).then_inc(S.dl, 16)
+
+    g.vector.memset(T.ident[:], 1.0).then_inc(S.one, 1)
+    g.wait_ge(S.one, 1)
+    g.affine_select(T.ident[:], T.ident[:], [[-1, D]], AluOpType.is_equal, 0.0, 0, 1).then_inc(S.idr, 1)
+    g.wait_ge(S.wl, 32)
+    sent = 0
+    for r, (a, dst) in enumerate(relays[me]):
+        on, off = topo.mask(core, a), topo.mask(a, cores[dst[0]])
+        pool = [on & ~off, on & off][r % 2]
+        _send(g, T, topo, core, a, me, _take(pool if pool else on, E_ON))
+        sent += E_ON
+    for k in direct[me]:
+        _send(g, T, topo, core, cores[k], me, _take(topo.mask(core, cores[k]), E_OFF))
+        sent += E_OFF
+    g.wait_ge(S.sent, sent)
+
+    te = g.tensor
+
+    def emit_dx(k):
+        idx, h = k // 2, k % 2
+        j = seq[idx][1]
+        te.wait_ge(GS[k % 2], k // 2 + 1)
+        if h == 0:
+            te.wait_ge(S.tc, idx + 1)
+        mm = te.matmul(ACC[h][:, 0:HF], w1t(j), T.gbuf[:, k * HF:(k + 1) * HF], idx == 0, idx == len(seq) - 1)
+        if idx == len(seq) - 1:
+            mm.then_inc(DD[h], 1)
+
+    te.wait_ge(S.idr, 1)
+    pending = None
+    for idx, (ph, j) in enumerate(seq):
+        if pending is not None and ph != seq[idx - 1][0] and sum(1 for p, _ in seq if p == seq[idx - 1][0]) == 1:
+            emit_dx(pending)
+            pending = None
+        if j == me:
+            te.wait_ge(S.wl, 32)
+        else:
+            te.wait_ge(S["arr%d" % j], E_OFF)
+        if idx > 0:
+            te.wait_ge(S.tc, idx)
+        te.transpose(T.pt[:, 0:D], w1(j), T.ident[:]).then_inc(S.tp, 1)
+        for h in range(2):
+            k = 2 * idx + h
+            if k == 0:
+                te.wait_ge(S.xl, 16)
+            if k >= 2:
+                te.wait_ge(MS[k % 2], k // 2)
+            te.matmul(Z[k % 2][:, 0:HF], w1(j), T.xs[:, h * HF:(h + 1) * HF], True, True).then_inc(ZS[k % 2], 1)
+            if k == 0:
+                te.wait_ge(S.dl, 16)
+            if k >= 2:
+                te.wait_ge(GS[k % 2], k // 2)
+            te.matmul(U[k % 2][:, 0:HF], w2(j), T.dys[:, h * HF:(h + 1) * HF], True, True).then_inc(US[k % 2], 1)
+            if pending is not None:
+                emit_dx(pending)
+            pending = k
+    emit_dx(pending)
+
+    ve = g.vector
+    for k in range(nu):
+        m = T.msk[:, (k % 2) * HF:(k % 2 + 1) * HF]
+        ve.wait_ge(ZS[k % 2], k // 2 + 1)
+        ve.tensor_scalar(m, Z[k % 2][:, 0:HF], 0.0, None, AluOpType.is_gt).then_inc(MS[k % 2], 1)
+        ve.wait_ge(US[k % 2], k // 2 + 1)
+        ve.wait_ge(MS[k % 2], k // 2 + 1)
+        ve.tensor_tensor(T.gbuf[:, k * HF:(k + 1) * HF], m, U[k % 2][:, 0:HF], AluOpType.mult).then_inc(GS[k % 2], 1)
+    ve.wait_ge(S.dd1, 1)
+    ve.tensor_copy(T.outb[:, HF:TK], T.acc1[:, 0:HF]).then_inc(S.ev1, 1)
+
+    sc = g.scalar
+    for idx, (ph, j) in enumerate(seq):
+        sc.wait_ge(S.tp, idx + 1)
+        sc.activation(w1t(j), T.pt[:, 0:D], ActivationFunctionType.Copy).then_inc(S.tc, 1)
+    sc.wait_ge(S.dd0, 1)
+    sc.activation(T.outb[:, 0:HF], T.acc0[:, 0:HF], ActivationFunctionType.Copy).then_inc(S.ev0, 1)
+    sc.wait_ge(S.ev0, 1)
+    sc.dma_start(T.dx[:, 0:HF], T.outb[:, 0:HF]).then_inc(S.st0, 16)
+    sc.wait_ge(S.st0, 16)
+
+    g.sync.wait_ge(S.ev1, 1)
+    g.sync.dma_start(T.dx[:, HF:TK], T.outb[:, HF:TK]).then_inc(S.st1, 16)
+    g.sync.wait_ge(S.st1, 16)

@@ -11,20 +11,20 @@ E_OFF = 8
 
 SCRATCH = {
     "wall": ("sbuf", [128, NR * WB], "bfloat16"),
-    "xs": ("sbuf", [128, TK], "bfloat16"),
-    "dys": ("sbuf", [128, TK], "bfloat16"),
+    "xd": ("sbuf", [128, 2 * TK], "bfloat16"),
     "ident": ("sbuf", [128, D], "bfloat16"),
     "w1t": ("sbuf", [128, NR * D], "bfloat16"),
     "msk": ("sbuf", [128, 2 * HF], "bfloat16"),
     "gbuf": ("sbuf", [128, 2 * NR * HF], "bfloat16"),
+    "part": ("sbuf", [128, TK], "bfloat16"),
     "outb": ("sbuf", [128, TK], "bfloat16"),
     "z0": ("psum", [128, 512], "float32"), "z1": ("psum", [128, 512], "float32"),
     "u0": ("psum", [128, 512], "float32"), "u1": ("psum", [128, 512], "float32"),
     "acc0": ("psum", [128, 512], "float32"), "acc1": ("psum", [128, 512], "float32"),
     "pt": ("psum", [128, 1024], "bfloat16"),
 }
-SEMAPHORES = (["wl", "xl", "dl", "one", "idr", "sent", "zs0", "zs1", "us0", "us1", "ms0", "ms1", "gs0", "gs1",
-               "tp", "tc", "dd0", "dd1", "ev0", "ev1", "st0", "st1"] + ["arr%d" % j for j in range(NR)])
+SEMAPHORES = (["wl", "xl", "dl", "xa", "one", "idr", "sent", "zs0", "zs1", "us0", "us1", "ms0", "ms1", "gs0", "gs1",
+               "tp", "tc", "dd0", "dd1", "ev0", "ev1", "pa0", "pa1", "st0", "st1"] + ["arr%d" % j for j in range(NR)])
 
 
 def _take(mask, n):
@@ -64,73 +64,43 @@ def _plan(cores, topo):
             for p, k in enumerate(dst):
                 keys[k].append(((2, p, 0 if die == topo.die(c) else 1), i))
         relays.append(rl)
-    order = []
+    order, helper = [], []
     for d in range(n):
-        order.append([(0, d)] + [(key[0], j) for key, j in sorted(keys[d])])
-    return direct, relays, order
+        full = [(key[0], j) for key, j in sorted(keys[d])]
+        group = [ph for ph, _ in full if sum(1 for p, _ in full if p == ph) >= 2][0]
+        hb = [j for ph, j in full if ph == group][1]
+        hc = sorted(relays[d], key=lambda r: topo.die(r[0]) != topo.die(cores[d]))[0][0]
+        helper.append((hc, hb))
+        order.append([(0, d)] + [(ph, j) for ph, j in full if j != hb])
+    return direct, relays, order, helper
 
 
-def _send(g, T, topo, src, dst, j, mask):
+def _write(g, T, topo, src, dst, ap, sem, mask):
     rid, pid = topo.addr(dst, src)
-    blk = T.wall[:, j * WB:(j + 1) * WB]
-    g.remote_dma(out_ap=blk, in_ap=blk, remote_sem=T.sem["arr%d" % j], local_sem=T.sem.sent,
-                 pid=pid, routing_id=rid, dma_engine_mask=mask)
+    g.remote_dma(out_ap=ap, in_ap=ap, remote_sem=sem, local_sem=T.sem.sent, pid=pid, routing_id=rid, dma_engine_mask=mask)
 
 
-def rank_program(g, core, T, topo):
-    cores = list(T.cores)
-    direct, relays, order = _plan(cores, topo)
+def _blk(T, j):
+    return T.wall[:, j * WB:(j + 1) * WB]
+
+
+def _pipeline(g, T, seq, arrive, xw, dw):
     S = T.sem
-
-    for i in range(NR):
-        for a, dst in relays[i]:
-            if a == core:
-                g.wait_ge(S["arr%d" % i], E_ON)
-                for k in dst:
-                    _send(g, T, topo, core, cores[k], i, _take(topo.mask(core, cores[k]), E_OFF))
-                g.wait_ge(S.sent, E_OFF * len(dst))
-    me = T.rank_of(core)
-    if me is None:
-        return
-
     w1 = lambda j: T.wall[:, j * WB:j * WB + D]
     w2 = lambda j: T.wall[:, j * WB + D:(j + 1) * WB]
     w1t = lambda j: T.w1t[:, j * D:(j + 1) * D]
     Z, U, ACC = [T.z0, T.z1], [T.u0, T.u1], [T.acc0, T.acc1]
     ZS, US, MS, GS, DD = [S.zs0, S.zs1], [S.us0, S.us1], [S.ms0, S.ms1], [S.gs0, S.gs1], [S.dd0, S.dd1]
-    seq = order[me]
-    nu = 2 * len(seq)
-
-    g.sync.dma_start(w1(me), T.w1[:]).then_inc(S.wl, 16)
-    g.scalar.dma_start(w2(me), T.w2t[:]).then_inc(S.wl, 16)
-    g.sync.dma_start(T.xs[:], T.x[:]).then_inc(S.xl, 16)
-    g.scalar.dma_start(T.dys[:], T.dy[:]).then_inc(S.dl, 16)
-
-    g.vector.memset(T.ident[:], 1.0).then_inc(S.one, 1)
-    g.wait_ge(S.one, 1)
-    g.affine_select(T.ident[:], T.ident[:], [[-1, D]], AluOpType.is_equal, 0.0, 0, 1).then_inc(S.idr, 1)
-    g.wait_ge(S.wl, 32)
-    sent = 0
-    for r, (a, dst) in enumerate(relays[me]):
-        on, off = topo.mask(core, a), topo.mask(a, cores[dst[0]])
-        pool = [on & ~off, on & off][r % 2]
-        _send(g, T, topo, core, a, me, _take(pool if pool else on, E_ON))
-        sent += E_ON
-    for k in direct[me]:
-        _send(g, T, topo, core, cores[k], me, _take(topo.mask(core, cores[k]), E_OFF))
-        sent += E_OFF
-    g.wait_ge(S.sent, sent)
-
-    te = g.tensor
+    te, ve, sc = g.tensor, g.vector, g.scalar
+    last = len(seq) - 1
 
     def emit_dx(k):
         idx, h = k // 2, k % 2
-        j = seq[idx][1]
         te.wait_ge(GS[k % 2], k // 2 + 1)
         if h == 0:
             te.wait_ge(S.tc, idx + 1)
-        mm = te.matmul(ACC[h][:, 0:HF], w1t(j), T.gbuf[:, k * HF:(k + 1) * HF], idx == 0, idx == len(seq) - 1)
-        if idx == len(seq) - 1:
+        mm = te.matmul(ACC[h][:, 0:HF], w1t(seq[idx][1]), T.gbuf[:, k * HF:(k + 1) * HF], idx == 0, idx == last)
+        if idx == last:
             mm.then_inc(DD[h], 1)
 
     te.wait_ge(S.idr, 1)
@@ -139,51 +109,119 @@ def rank_program(g, core, T, topo):
         if pending is not None and ph != seq[idx - 1][0] and sum(1 for p, _ in seq if p == seq[idx - 1][0]) == 1:
             emit_dx(pending)
             pending = None
-        if j == me:
-            te.wait_ge(S.wl, 32)
-        else:
-            te.wait_ge(S["arr%d" % j], E_OFF)
+        te.wait_ge(arrive[j][0], arrive[j][1])
         if idx > 0:
             te.wait_ge(S.tc, idx)
         te.transpose(T.pt[:, 0:D], w1(j), T.ident[:]).then_inc(S.tp, 1)
         for h in range(2):
             k = 2 * idx + h
             if k == 0:
-                te.wait_ge(S.xl, 16)
+                te.wait_ge(xw[0], xw[1])
             if k >= 2:
                 te.wait_ge(MS[k % 2], k // 2)
-            te.matmul(Z[k % 2][:, 0:HF], w1(j), T.xs[:, h * HF:(h + 1) * HF], True, True).then_inc(ZS[k % 2], 1)
+            te.matmul(Z[k % 2][:, 0:HF], w1(j), T.xd[:, h * HF:(h + 1) * HF], True, True).then_inc(ZS[k % 2], 1)
             if k == 0:
-                te.wait_ge(S.dl, 16)
+                te.wait_ge(dw[0], dw[1])
             if k >= 2:
                 te.wait_ge(GS[k % 2], k // 2)
-            te.matmul(U[k % 2][:, 0:HF], w2(j), T.dys[:, h * HF:(h + 1) * HF], True, True).then_inc(US[k % 2], 1)
+            te.matmul(U[k % 2][:, 0:HF], w2(j), T.xd[:, TK + h * HF:TK + (h + 1) * HF], True, True).then_inc(US[k % 2], 1)
             if pending is not None:
                 emit_dx(pending)
             pending = k
     emit_dx(pending)
 
-    ve = g.vector
-    for k in range(nu):
+    for k in range(2 * len(seq)):
         m = T.msk[:, (k % 2) * HF:(k % 2 + 1) * HF]
         ve.wait_ge(ZS[k % 2], k // 2 + 1)
         ve.tensor_scalar(m, Z[k % 2][:, 0:HF], 0.0, None, AluOpType.is_gt).then_inc(MS[k % 2], 1)
         ve.wait_ge(US[k % 2], k // 2 + 1)
         ve.wait_ge(MS[k % 2], k // 2 + 1)
         ve.tensor_tensor(T.gbuf[:, k * HF:(k + 1) * HF], m, U[k % 2][:, 0:HF], AluOpType.mult).then_inc(GS[k % 2], 1)
-    ve.wait_ge(S.dd1, 1)
-    ve.tensor_copy(T.outb[:, HF:TK], T.acc1[:, 0:HF]).then_inc(S.ev1, 1)
 
-    sc = g.scalar
     for idx, (ph, j) in enumerate(seq):
         sc.wait_ge(S.tp, idx + 1)
         sc.activation(w1t(j), T.pt[:, 0:D], ActivationFunctionType.Copy).then_inc(S.tc, 1)
-    sc.wait_ge(S.dd0, 1)
-    sc.activation(T.outb[:, 0:HF], T.acc0[:, 0:HF], ActivationFunctionType.Copy).then_inc(S.ev0, 1)
-    sc.wait_ge(S.ev0, 1)
-    sc.dma_start(T.dx[:, 0:HF], T.outb[:, 0:HF]).then_inc(S.st0, 16)
-    sc.wait_ge(S.st0, 16)
 
+
+def _identity(g, T):
+    g.vector.memset(T.ident[:], 1.0).then_inc(T.sem.one, 1)
+    g.wait_ge(T.sem.one, 1)
+    g.affine_select(T.ident[:], T.ident[:], [[-1, D]], AluOpType.is_equal, 0.0, 0, 1).then_inc(T.sem.idr, 1)
+
+
+def rank_program(g, core, T, topo):
+    cores = list(T.cores)
+    direct, relays, order, helper = _plan(cores, topo)
+    S = T.sem
+    arr = lambda j: S["arr%d" % j]
+    tgt = lambda j, d: helper[d][0] if helper[d][1] == j else cores[d]
+    halves = [(T.part[:, 0:HF], S.pa0), (T.part[:, HF:TK], S.pa1)]
+
+    for i in range(NR):
+        for a, dst in relays[i]:
+            if a != core:
+                continue
+            helps = helper[i][0] == core
+            if helps:
+                _identity(g, T)
+            g.wait_ge(arr(i), E_ON)
+            sent = 0
+            for k in dst:
+                t = tgt(i, k)
+                _write(g, T, topo, core, t, _blk(T, i), arr(i), _take(topo.mask(core, t), E_OFF))
+                sent += E_OFF
+            if helps:
+                hb = helper[i][1]
+                _pipeline(g, T, [(0, hb)], {hb: (arr(hb), E_OFF)}, (S.xa, E_ON), (S.xa, E_ON))
+                g.scalar.wait_ge(S.dd0, 1)
+                g.scalar.activation(halves[0][0], T.acc0[:, 0:HF], ActivationFunctionType.Copy).then_inc(S.ev0, 1)
+                g.vector.wait_ge(S.dd1, 1)
+                g.vector.tensor_copy(halves[1][0], T.acc1[:, 0:HF]).then_inc(S.ev1, 1)
+                for (ap, sem), ev in zip(halves, [S.ev0, S.ev1]):
+                    g.wait_ge(ev, 1)
+                    _write(g, T, topo, core, cores[i], ap, sem, _take(topo.mask(core, cores[i]), E_ON))
+                    sent += E_ON
+            g.wait_ge(S.sent, sent)
+    me = T.rank_of(core)
+    if me is None:
+        return
+
+    g.sync.dma_start(T.wall[:, me * WB:me * WB + D], T.w1[:]).then_inc(S.wl, 16)
+    g.scalar.dma_start(T.wall[:, me * WB + D:(me + 1) * WB], T.w2t[:]).then_inc(S.wl, 16)
+    g.sync.dma_start(T.xd[:, 0:TK], T.x[:]).then_inc(S.xl, 16)
+    g.scalar.dma_start(T.xd[:, TK:2 * TK], T.dy[:]).then_inc(S.dl, 16)
+
+    _identity(g, T)
+    g.wait_ge(S.wl, 32)
+    sent = 0
+    hc = helper[me][0]
+    stay = topo.mask(core, hc) & ~topo.mask(hc, cores[relays[me][0][1][0]])
+    for r, (a, dst) in enumerate(relays[me]):
+        pool = [stay, topo.mask(core, a) & ~stay][r % 2]
+        _write(g, T, topo, core, a, _blk(T, me), arr(me), _take(pool if pool else topo.mask(core, a), E_ON))
+        sent += E_ON
+    for p, k in enumerate(direct[me]):
+        t = tgt(me, k)
+        _write(g, T, topo, core, t, _blk(T, me), arr(me), _take(topo.mask(core, t), E_OFF))
+        sent += E_OFF
+        if p == 0:
+            g.wait_ge(S.xl, 16)
+            g.wait_ge(S.dl, 16)
+            _write(g, T, topo, core, hc, T.xd[:], S.xa, _take(stay if stay else topo.mask(core, hc), E_ON))
+            sent += E_ON
+    g.wait_ge(S.sent, sent)
+
+    arrive = {j: (arr(j), E_OFF) for _, j in order[me]}
+    arrive[me] = (S.wl, 32)
+    _pipeline(g, T, order[me], arrive, (S.xl, 16), (S.dl, 16))
+
+    for h, (acc, dd, ev) in enumerate([(T.acc0, S.dd0, S.ev0), (T.acc1, S.dd1, S.ev1)]):
+        g.vector.wait_ge(dd, 1)
+        g.vector.wait_ge(halves[h][1], E_ON)
+        g.vector.tensor_tensor(T.outb[:, h * HF:(h + 1) * HF], acc[:, 0:HF], halves[h][0], AluOpType.add).then_inc(ev, 1)
+    g.scalar.wait_ge(S.ev0, 1)
+    g.scalar.dma_start(T.dx[:, 0:HF], T.outb[:, 0:HF]).then_inc(S.st0, 16)
+    g.scalar.wait_ge(S.st0, 16)
     g.sync.wait_ge(S.ev1, 1)
     g.sync.dma_start(T.dx[:, HF:TK], T.outb[:, HF:TK]).then_inc(S.st1, 16)
     g.sync.wait_ge(S.st1, 16)

@@ -1,3 +1,4 @@
+from concourse.bass import DstId, RemoteDMATransfer
 from concourse.mybir import AluOpType, ActivationFunctionType
 
 SIM_CORES = 256
@@ -6,25 +7,28 @@ D = 128
 TK = 512
 HF = 256
 WB = 2 * D
+NH = 2
 E_ON = 8
 E_OFF = 8
 
 SCRATCH = {
+    "wd": ("dram", [128, WB], "bfloat16"),
     "wall": ("sbuf", [128, NR * WB], "bfloat16"),
     "xd": ("sbuf", [128, 2 * TK], "bfloat16"),
     "ident": ("sbuf", [128, D], "bfloat16"),
     "w1t": ("sbuf", [128, NR * D], "bfloat16"),
     "msk": ("sbuf", [128, 2 * HF], "bfloat16"),
     "gbuf": ("sbuf", [128, 2 * NR * HF], "bfloat16"),
-    "part": ("sbuf", [128, TK], "bfloat16"),
+    "part0": ("sbuf", [128, TK], "bfloat16"),
+    "part1": ("sbuf", [128, TK], "bfloat16"),
     "outb": ("sbuf", [128, TK], "bfloat16"),
     "z0": ("psum", [128, 512], "float32"), "z1": ("psum", [128, 512], "float32"),
     "u0": ("psum", [128, 512], "float32"), "u1": ("psum", [128, 512], "float32"),
     "acc0": ("psum", [128, 512], "float32"), "acc1": ("psum", [128, 512], "float32"),
     "pt": ("psum", [128, 1024], "bfloat16"),
 }
-SEMAPHORES = (["wl", "xl", "dl", "xa", "one", "idr", "sent", "zs0", "zs1", "us0", "us1", "ms0", "ms1", "gs0", "gs1",
-               "tp", "tc", "dd0", "dd1", "ev0", "ev1", "pa0", "pa1", "st0", "st1"] + ["arr%d" % j for j in range(NR)])
+SEMAPHORES = (["wdl", "wl", "xl", "dl", "xa", "one", "idr", "ida", "sent", "zs0", "zs1", "us0", "us1", "ms0", "ms1", "gs0", "gs1",
+               "tp", "tc", "dd0", "dd1", "ev0", "ev1", "p00", "p01", "p10", "p11", "st0", "st1"] + ["arr%d" % j for j in range(NR)])
 
 
 def _take(mask, n):
@@ -41,7 +45,7 @@ def _take(mask, n):
 
 def _plan(cores, topo):
     n = len(cores)
-    direct, relays, keys = [], [], [[] for _ in range(n)]
+    direct, relays, keys, spare = [], [], [[] for _ in range(n)], []
     for i, c in enumerate(cores):
         rot = sorted((k for k in range(n) if k != i), key=lambda k: (k - i) % n)
         dr = [k for k in rot if topo.may_write(c, cores[k])]
@@ -50,8 +54,8 @@ def _plan(cores, topo):
         for p, k in enumerate(dr):
             keys[k].append(((1, p, 0), i))
         q = sorted(dr + [i]).index(i)
-        mine = [a for a in range(SIM_CORES) if a not in cores and topo.host(a) == topo.host(c) and topo.chip(a) == topo.chip(c)
-                and all(topo.may_write(a, cores[k]) for k in cr)]
+        chipm = [a for a in range(SIM_CORES) if a not in cores and topo.host(a) == topo.host(c) and topo.chip(a) == topo.chip(c)]
+        mine = [a for a in chipm if all(topo.may_write(a, cores[k]) for k in cr)]
         dies = [topo.die(c)] + sorted(set(topo.die(a) for a in mine if topo.die(a) != topo.die(c)))
         nrel = (len(cr) + 1) // 2
         rl, used = [], []
@@ -64,27 +68,30 @@ def _plan(cores, topo):
             for p, k in enumerate(dst):
                 keys[k].append(((2, p, 0 if die == topo.die(c) else 1), i))
         relays.append(rl)
+        spare.append([a for a in chipm if a not in used and topo.die(a) == topo.die(c)])
     order, helper = [], []
     for d in range(n):
         full = [(key[0], j) for key, j in sorted(keys[d])]
         group = [ph for ph, _ in full if sum(1 for p, _ in full if p == ph) >= 2][0]
-        hb = [j for ph, j in full if ph == group][1]
-        hc = sorted(relays[d], key=lambda r: topo.die(r[0]) != topo.die(cores[d]))[0][0]
-        helper.append((hc, hb))
-        order.append([(0, d)] + [(ph, j) for ph, j in full if j != hb])
+        cand = [j for ph, j in full if ph == group]
+        hb = cand[0:NH] if len(cand) > NH + 1 else cand[1:NH + 1]
+        hc = [a for a, _ in sorted(relays[d], key=lambda r: topo.die(r[0]) != topo.die(cores[d]))][0:NH]
+        hc = spare[d][0:NH - len(hc)] + hc
+        helper.append(list(zip(hc, hb)))
+        order.append([(0, d)] + [(ph, j) for ph, j in full if j not in hb])
     return direct, relays, order, helper
 
 
-def _write(g, T, topo, src, dst, ap, sem, mask):
+def _write(g, T, topo, src, dst, out_ap, in_ap, sem, mask):
     rid, pid = topo.addr(dst, src)
-    g.remote_dma(out_ap=ap, in_ap=ap, remote_sem=sem, local_sem=T.sem.sent, pid=pid, routing_id=rid, dma_engine_mask=mask)
+    g.remote_dma(out_ap=out_ap, in_ap=in_ap, remote_sem=sem, local_sem=T.sem.sent, pid=pid, routing_id=rid, dma_engine_mask=mask)
 
 
 def _blk(T, j):
     return T.wall[:, j * WB:(j + 1) * WB]
 
 
-def _pipeline(g, T, seq, arrive, xw, dw):
+def _pipeline(g, T, seq, arrive, xw, dw, idw, extra):
     S = T.sem
     w1 = lambda j: T.wall[:, j * WB:j * WB + D]
     w2 = lambda j: T.wall[:, j * WB + D:(j + 1) * WB]
@@ -99,11 +106,11 @@ def _pipeline(g, T, seq, arrive, xw, dw):
         te.wait_ge(GS[k % 2], k // 2 + 1)
         if h == 0:
             te.wait_ge(S.tc, idx + 1)
-        mm = te.matmul(ACC[h][:, 0:HF], w1t(seq[idx][1]), T.gbuf[:, k * HF:(k + 1) * HF], idx == 0, idx == last)
-        if idx == last:
+        mm = te.matmul(ACC[h][:, 0:HF], w1t(seq[idx][1]), T.gbuf[:, k * HF:(k + 1) * HF], idx == 0, idx == last and extra is None)
+        if idx == last and extra is None:
             mm.then_inc(DD[h], 1)
 
-    te.wait_ge(S.idr, 1)
+    te.wait_ge(idw[0], idw[1])
     pending = None
     for idx, (ph, j) in enumerate(seq):
         if pending is not None and ph != seq[idx - 1][0] and sum(1 for p, _ in seq if p == seq[idx - 1][0]) == 1:
@@ -129,6 +136,10 @@ def _pipeline(g, T, seq, arrive, xw, dw):
                 emit_dx(pending)
             pending = k
     emit_dx(pending)
+    if extra is not None:
+        for h, (ap, sem, cnt) in enumerate(extra):
+            te.wait_ge(sem, cnt)
+            te.matmul(ACC[h][:, 0:HF], T.ident[:], ap, False, True).then_inc(DD[h], 1)
 
     for k in range(2 * len(seq)):
         m = T.msk[:, (k % 2) * HF:(k % 2 + 1) * HF]
@@ -143,82 +154,103 @@ def _pipeline(g, T, seq, arrive, xw, dw):
         sc.activation(w1t(j), T.pt[:, 0:D], ActivationFunctionType.Copy).then_inc(S.tc, 1)
 
 
-def _identity(g, T):
-    g.vector.memset(T.ident[:], 1.0).then_inc(T.sem.one, 1)
-    g.wait_ge(T.sem.one, 1)
-    g.affine_select(T.ident[:], T.ident[:], [[-1, D]], AluOpType.is_equal, 0.0, 0, 1).then_inc(T.sem.idr, 1)
-
-
 def rank_program(g, core, T, topo):
     cores = list(T.cores)
     direct, relays, order, helper = _plan(cores, topo)
     S = T.sem
     arr = lambda j: S["arr%d" % j]
-    tgt = lambda j, d: helper[d][0] if helper[d][1] == j else cores[d]
-    halves = [(T.part[:, 0:HF], S.pa0), (T.part[:, HF:TK], S.pa1)]
+
+    def tgt(j, d):
+        for a, b in helper[d]:
+            if b == j:
+                return a
+        return cores[d]
+
+    def halves(s):
+        buf = T["part%d" % s]
+        return [(buf[:, 0:HF], S["p%d0" % s]), (buf[:, HF:TK], S["p%d1" % s])]
 
     for i in range(NR):
-        for a, dst in relays[i]:
-            if a != core:
-                continue
-            helps = helper[i][0] == core
-            if helps:
-                _identity(g, T)
+        dst = [dl for a, dl in relays[i] if a == core]
+        hs = [s for s, (a, _) in enumerate(helper[i]) if a == core]
+        if not dst and not hs:
+            continue
+        sent = 0
+        if dst:
             g.wait_ge(arr(i), E_ON)
-            sent = 0
-            for k in dst:
+            for k in dst[0]:
                 t = tgt(i, k)
-                _write(g, T, topo, core, t, _blk(T, i), arr(i), _take(topo.mask(core, t), E_OFF))
+                _write(g, T, topo, core, t, _blk(T, i), T.wd[:], arr(i), _take(topo.mask(core, t), E_OFF))
                 sent += E_OFF
-            if helps:
-                hb = helper[i][1]
-                _pipeline(g, T, [(0, hb)], {hb: (arr(hb), E_OFF)}, (S.xa, E_ON), (S.xa, E_ON))
-                g.scalar.wait_ge(S.dd0, 1)
-                g.scalar.activation(halves[0][0], T.acc0[:, 0:HF], ActivationFunctionType.Copy).then_inc(S.ev0, 1)
-                g.vector.wait_ge(S.dd1, 1)
-                g.vector.tensor_copy(halves[1][0], T.acc1[:, 0:HF]).then_inc(S.ev1, 1)
-                for (ap, sem), ev in zip(halves, [S.ev0, S.ev1]):
-                    g.wait_ge(ev, 1)
-                    _write(g, T, topo, core, cores[i], ap, sem, _take(topo.mask(core, cores[i]), E_ON))
-                    sent += E_ON
-            g.wait_ge(S.sent, sent)
+        if hs:
+            s = hs[0]
+            hb = helper[i][s][1]
+            hv = halves(s)
+            _pipeline(g, T, [(0, hb)], {hb: (arr(hb), E_OFF)}, (S.xa, E_ON), (S.xa, E_ON), (S.ida, E_ON), None)
+            g.scalar.wait_ge(S.dd0, 1)
+            g.scalar.activation(hv[0][0], T.acc0[:, 0:HF], ActivationFunctionType.Copy).then_inc(S.ev0, 1)
+            g.vector.wait_ge(S.dd1, 1)
+            g.vector.tensor_copy(hv[1][0], T.acc1[:, 0:HF]).then_inc(S.ev1, 1)
+            for (ap, sem), ev in zip(hv, [S.ev0, S.ev1]):
+                g.wait_ge(ev, 1)
+                _write(g, T, topo, core, cores[i], ap, ap, sem, _take(topo.mask(core, cores[i]), E_ON))
+                sent += E_ON
+        g.wait_ge(S.sent, sent)
     me = T.rank_of(core)
     if me is None:
         return
 
-    g.sync.dma_start(T.wall[:, me * WB:me * WB + D], T.w1[:]).then_inc(S.wl, 16)
-    g.scalar.dma_start(T.wall[:, me * WB + D:(me + 1) * WB], T.w2t[:]).then_inc(S.wl, 16)
+    g.sync.dma_start(T.wd[:, 0:D], T.w1[:]).then_inc(S.wdl, 16)
+    g.scalar.dma_start(T.wd[:, D:WB], T.w2t[:]).then_inc(S.wdl, 16)
     g.sync.dma_start(T.xd[:, 0:TK], T.x[:]).then_inc(S.xl, 16)
     g.scalar.dma_start(T.xd[:, TK:2 * TK], T.dy[:]).then_inc(S.dl, 16)
+    g.sync.dma_start(T.wall[:, me * WB:me * WB + D], T.w1[:]).then_inc(S.wl, 16)
+    g.scalar.dma_start(T.wall[:, me * WB + D:(me + 1) * WB], T.w2t[:]).then_inc(S.wl, 16)
 
-    _identity(g, T)
-    g.wait_ge(S.wl, 32)
+    hcs = [a for a, _ in helper[me]]
+    on = topo.mask(core, hcs[0])
+    stay = on & ~topo.mask(core, cores[direct[me][0]])
+    if not stay:
+        stay = on
+    other = on & ~stay if on & ~stay else on
     sent = 0
-    hc = helper[me][0]
-    stay = topo.mask(core, hc) & ~topo.mask(hc, cores[relays[me][0][1][0]])
+    g.vector.memset(T.ident[:], 1.0).then_inc(S.one, 1)
+    g.wait_ge(S.one, 1)
+    g.affine_select(T.ident[:], T.ident[:], [[-1, D]], AluOpType.is_equal, 0.0, 0, 1).then_inc(S.idr, 1)
+    g.wait_ge(S.idr, 1)
+    ids = []
+    for a in hcs:
+        rid, pid = topo.addr(a, core)
+        ids.append(DstId(rid=rid, pnc=pid))
+    g.remote_dma_fused([RemoteDMATransfer(dst_ids=ids, dma_engine_mask=_take(stay, E_ON), remote_sem=S.ida,
+                                          srcs=[T.ident[:]], dsts=[T.ident[:] for _ in hcs])], local_sem=S.sent)
+    sent += E_ON
+    g.wait_ge(S.wdl, 32)
     for r, (a, dst) in enumerate(relays[me]):
-        pool = [stay, topo.mask(core, a) & ~stay][r % 2]
-        _write(g, T, topo, core, a, _blk(T, me), arr(me), _take(pool if pool else topo.mask(core, a), E_ON))
+        _write(g, T, topo, core, a, T.wd[:], T.wd[:], arr(me), _take([stay, other][r % 2], E_ON))
         sent += E_ON
     for p, k in enumerate(direct[me]):
         t = tgt(me, k)
-        _write(g, T, topo, core, t, _blk(T, me), arr(me), _take(topo.mask(core, t), E_OFF))
+        _write(g, T, topo, core, t, _blk(T, me), T.wd[:], arr(me), _take(topo.mask(core, t), E_OFF))
         sent += E_OFF
         if p == 0:
             g.wait_ge(S.xl, 16)
             g.wait_ge(S.dl, 16)
-            _write(g, T, topo, core, hc, T.xd[:], S.xa, _take(stay if stay else topo.mask(core, hc), E_ON))
+            _write(g, T, topo, core, hcs[0], T.xd[:], T.xd[:], S.xa, _take(stay, E_ON))
             sent += E_ON
+    _write(g, T, topo, core, hcs[1], T.xd[:], T.xd[:], S.xa, _take(other, E_ON))
+    sent += E_ON
     g.wait_ge(S.sent, sent)
 
     arrive = {j: (arr(j), E_OFF) for _, j in order[me]}
     arrive[me] = (S.wl, 32)
-    _pipeline(g, T, order[me], arrive, (S.xl, 16), (S.dl, 16))
+    _pipeline(g, T, order[me], arrive, (S.xl, 16), (S.dl, 16), (S.idr, 1), [(ap, sem, E_ON) for ap, sem in halves(0)])
 
+    hv = halves(1)
     for h, (acc, dd, ev) in enumerate([(T.acc0, S.dd0, S.ev0), (T.acc1, S.dd1, S.ev1)]):
         g.vector.wait_ge(dd, 1)
-        g.vector.wait_ge(halves[h][1], E_ON)
-        g.vector.tensor_tensor(T.outb[:, h * HF:(h + 1) * HF], acc[:, 0:HF], halves[h][0], AluOpType.add).then_inc(ev, 1)
+        g.vector.wait_ge(hv[h][1], E_ON)
+        g.vector.tensor_tensor(T.outb[:, h * HF:(h + 1) * HF], acc[:, 0:HF], hv[h][0], AluOpType.add).then_inc(ev, 1)
     g.scalar.wait_ge(S.ev0, 1)
     g.scalar.dma_start(T.dx[:, 0:HF], T.outb[:, 0:HF]).then_inc(S.st0, 16)
     g.scalar.wait_ge(S.st0, 16)

from concourse.bass import DstId, RemoteDMATransfer
from concourse.mybir import AluOpType, ActivationFunctionType

SIM_CORES = 256
NR = 6
D = 128
TK = 512
HF = 256
WB = 2 * D
NH = 2
E_ON = 8
E_OFF = 8

SCRATCH = {
    "wd": ("dram", [128, WB], "bfloat16"),
    "wall": ("sbuf", [128, NR * WB], "bfloat16"),
    "xd": ("sbuf", [128, 2 * TK], "bfloat16"),
    "ident": ("sbuf", [128, D], "bfloat16"),
    "w1t": ("sbuf", [128, NR * D], "bfloat16"),
    "msk": ("sbuf", [128, 2 * HF], "bfloat16"),
    "gbuf": ("sbuf", [128, 2 * NR * HF], "bfloat16"),
    "part0": ("sbuf", [128, TK], "bfloat16"),
    "part1": ("sbuf", [128, TK], "bfloat16"),
    "outb": ("sbuf", [128, TK], "bfloat16"),
    "z0": ("psum", [128, 512], "float32"), "z1": ("psum", [128, 512], "float32"),
    "u0": ("psum", [128, 512], "float32"), "u1": ("psum", [128, 512], "float32"),
    "acc0": ("psum", [128, 512], "float32"), "acc1": ("psum", [128, 512], "float32"),
    "pt": ("psum", [128, 1024], "bfloat16"),
}
SEMAPHORES = (["wdl", "wl", "xl", "dl", "xa", "one", "idr", "ida", "sent", "zs0", "zs1", "us0", "us1", "ms0", "ms1", "gs0", "gs1",
               "tp", "tc", "dd0", "dd1", "ev0", "ev1", "p00", "p01", "p10", "p11", "st0", "st1"] + ["arr%d" % j for j in range(NR)])


def _take(mask, n):
    out, got, e = 0, 0, 0
    while got < n:
        if (mask >> e) & 1:
            out |= 1 << e
            got += 1
        e += 1
        if e > 64:
            raise ValueError("mask too small")
    return out


def _plan(cores, topo):
    n = len(cores)
    direct, relays, keys, spare = [], [], [[] for _ in range(n)], []
    for i, c in enumerate(cores):
        rot = sorted((k for k in range(n) if k != i), key=lambda k: (k - i) % n)
        dr = [k for k in rot if topo.may_write(c, cores[k])]
        cr = [k for k in rot if not topo.may_write(c, cores[k])]
        direct.append(dr)
        for p, k in enumerate(dr):
            keys[k].append(((1, p, 0), i))
        q = sorted(dr + [i]).index(i)
        chipm = [a for a in range(SIM_CORES) if a not in cores and topo.host(a) == topo.host(c) and topo.chip(a) == topo.chip(c)]
        mine = [a for a in chipm if all(topo.may_write(a, cores[k]) for k in cr)]
        dies = [topo.die(c)] + sorted(set(topo.die(a) for a in mine if topo.die(a) != topo.die(c)))
        nrel = (len(cr) + 1) // 2
        rl, used = [], []
        for r in range(nrel):
            die = dies[(r + q) % len(dies)]
            a = [a for a in mine if topo.die(a) == die and a not in used][0]
            used.append(a)
            dst = cr[r::nrel]
            rl.append((a, dst))
            for p, k in enumerate(dst):
                keys[k].append(((2, p, 0 if die == topo.die(c) else 1), i))
        relays.append(rl)
        spare.append([a for a in chipm if a not in used and topo.die(a) == topo.die(c)])
    order, helper = [], []
    for d in range(n):
        full = [(key[0], j) for key, j in sorted(keys[d])]
        group = [ph for ph, _ in full if sum(1 for p, _ in full if p == ph) >= 2][0]
        cand = [j for ph, j in full if ph == group]
        hb = cand[0:NH] if len(cand) > NH + 1 else cand[1:NH + 1]
        hc = [a for a, _ in sorted(relays[d], key=lambda r: topo.die(r[0]) != topo.die(cores[d]))][0:NH]
        hc = spare[d][0:NH - len(hc)] + hc
        helper.append(list(zip(hc, hb)))
        order.append([(0, d)] + [(ph, j) for ph, j in full if j not in hb])
    return direct, relays, order, helper


def _write(g, T, topo, src, dst, out_ap, in_ap, sem, mask):
    rid, pid = topo.addr(dst, src)
    g.remote_dma(out_ap=out_ap, in_ap=in_ap, remote_sem=sem, local_sem=T.sem.sent, pid=pid, routing_id=rid, dma_engine_mask=mask)


def _blk(T, j):
    return T.wall[:, j * WB:(j + 1) * WB]


def _pipeline(g, T, seq, arrive, xw, dw, idw, extra):
    S = T.sem
    w1 = lambda j: T.wall[:, j * WB:j * WB + D]
    w2 = lambda j: T.wall[:, j * WB + D:(j + 1) * WB]
    w1t = lambda j: T.w1t[:, j * D:(j + 1) * D]
    Z, U, ACC = [T.z0, T.z1], [T.u0, T.u1], [T.acc0, T.acc1]
    ZS, US, MS, GS, DD = [S.zs0, S.zs1], [S.us0, S.us1], [S.ms0, S.ms1], [S.gs0, S.gs1], [S.dd0, S.dd1]
    te, ve, sc = g.tensor, g.vector, g.scalar
    last = len(seq) - 1

    def emit_dx(k):
        idx, h = k // 2, k % 2
        te.wait_ge(GS[k % 2], k // 2 + 1)
        if h == 0:
            te.wait_ge(S.tc, idx + 1)
        mm = te.matmul(ACC[h][:, 0:HF], w1t(seq[idx][1]), T.gbuf[:, k * HF:(k + 1) * HF], idx == 0, idx == last and extra is None)
        if idx == last and extra is None:
            mm.then_inc(DD[h], 1)

    te.wait_ge(idw[0], idw[1])
    pending = None
    for idx, (ph, j) in enumerate(seq):
        if pending is not None and ph != seq[idx - 1][0] and sum(1 for p, _ in seq if p == seq[idx - 1][0]) == 1:
            emit_dx(pending)
            pending = None
        te.wait_ge(arrive[j][0], arrive[j][1])
        if idx > 0:
            te.wait_ge(S.tc, idx)
        te.transpose(T.pt[:, 0:D], w1(j), T.ident[:]).then_inc(S.tp, 1)
        for h in range(2):
            k = 2 * idx + h
            if k == 0:
                te.wait_ge(xw[0], xw[1])
            if k >= 2:
                te.wait_ge(MS[k % 2], k // 2)
            te.matmul(Z[k % 2][:, 0:HF], w1(j), T.xd[:, h * HF:(h + 1) * HF], True, True).then_inc(ZS[k % 2], 1)
            if k == 0:
                te.wait_ge(dw[0], dw[1])
            if k >= 2:
                te.wait_ge(GS[k % 2], k // 2)
            te.matmul(U[k % 2][:, 0:HF], w2(j), T.xd[:, TK + h * HF:TK + (h + 1) * HF], True, True).then_inc(US[k % 2], 1)
            if pending is not None:
                emit_dx(pending)
            pending = k
    emit_dx(pending)
    if extra is not None:
        for h, (ap, sem, cnt) in enumerate(extra):
            te.wait_ge(sem, cnt)
            te.matmul(ACC[h][:, 0:HF], T.ident[:], ap, False, True).then_inc(DD[h], 1)

    for k in range(2 * len(seq)):
        m = T.msk[:, (k % 2) * HF:(k % 2 + 1) * HF]
        ve.wait_ge(ZS[k % 2], k // 2 + 1)
        ve.tensor_scalar(m, Z[k % 2][:, 0:HF], 0.0, None, AluOpType.is_gt).then_inc(MS[k % 2], 1)
        ve.wait_ge(US[k % 2], k // 2 + 1)
        ve.wait_ge(MS[k % 2], k // 2 + 1)
        ve.tensor_tensor(T.gbuf[:, k * HF:(k + 1) * HF], m, U[k % 2][:, 0:HF], AluOpType.mult).then_inc(GS[k % 2], 1)

    for idx, (ph, j) in enumerate(seq):
        sc.wait_ge(S.tp, idx + 1)
        sc.activation(w1t(j), T.pt[:, 0:D], ActivationFunctionType.Copy).then_inc(S.tc, 1)


def rank_program(g, core, T, topo):
    cores = list(T.cores)
    direct, relays, order, helper = _plan(cores, topo)
    S = T.sem
    arr = lambda j: S["arr%d" % j]

    def tgt(j, d):
        for a, b in helper[d]:
            if b == j:
                return a
        return cores[d]

    def halves(s):
        buf = T["part%d" % s]
        return [(buf[:, 0:HF], S["p%d0" % s]), (buf[:, HF:TK], S["p%d1" % s])]

    for i in range(NR):
        dst = [dl for a, dl in relays[i] if a == core]
        hs = [s for s, (a, _) in enumerate(helper[i]) if a == core]
        if not dst and not hs:
            continue
        sent = 0
        if dst:
            g.wait_ge(arr(i), E_ON)
            for k in dst[0]:
                t = tgt(i, k)
                _write(g, T, topo, core, t, _blk(T, i), T.wd[:], arr(i), _take(topo.mask(core, t), E_OFF))
                sent += E_OFF
        if hs:
            s = hs[0]
            hb = helper[i][s][1]
            hv = halves(s)
            _pipeline(g, T, [(0, hb)], {hb: (arr(hb), E_OFF)}, (S.xa, E_ON), (S.xa, E_ON), (S.ida, E_ON), None)
            g.scalar.wait_ge(S.dd0, 1)
            g.scalar.activation(hv[0][0], T.acc0[:, 0:HF], ActivationFunctionType.Copy).then_inc(S.ev0, 1)
            g.vector.wait_ge(S.dd1, 1)
            g.vector.tensor_copy(hv[1][0], T.acc1[:, 0:HF]).then_inc(S.ev1, 1)
            for (ap, sem), ev in zip(hv, [S.ev0, S.ev1]):
                g.wait_ge(ev, 1)
                _write(g, T, topo, core, cores[i], ap, ap, sem, _take(topo.mask(core, cores[i]), E_ON))
                sent += E_ON
        g.wait_ge(S.sent, sent)
    me = T.rank_of(core)
    if me is None:
        return

    g.sync.dma_start(T.wd[:, 0:D], T.w1[:]).then_inc(S.wdl, 16)
    g.scalar.dma_start(T.wd[:, D:WB], T.w2t[:]).then_inc(S.wdl, 16)
    g.sync.dma_start(T.xd[:, 0:TK], T.x[:]).then_inc(S.xl, 16)
    g.scalar.dma_start(T.xd[:, TK:2 * TK], T.dy[:]).then_inc(S.dl, 16)
    g.sync.dma_start(T.wall[:, me * WB:me * WB + D], T.w1[:]).then_inc(S.wl, 16)
    g.scalar.dma_start(T.wall[:, me * WB + D:(me + 1) * WB], T.w2t[:]).then_inc(S.wl, 16)

    hcs = [a for a, _ in helper[me]]
    on = topo.mask(core, hcs[0])
    stay = on & ~topo.mask(core, cores[direct[me][0]])
    if not stay:
        stay = on
    other = on & ~stay if on & ~stay else on
    sent = 0
    g.vector.memset(T.ident[:], 1.0).then_inc(S.one, 1)
    g.wait_ge(S.one, 1)
    g.affine_select(T.ident[:], T.ident[:], [[-1, D]], AluOpType.is_equal, 0.0, 0, 1).then_inc(S.idr, 1)
    g.wait_ge(S.idr, 1)
    ids = []
    for a in hcs:
        rid, pid = topo.addr(a, core)
        ids.append(DstId(rid=rid, pnc=pid))
    g.remote_dma_fused([RemoteDMATransfer(dst_ids=ids, dma_engine_mask=_take(stay, E_ON), remote_sem=S.ida,
                                          srcs=[T.ident[:]], dsts=[T.ident[:] for _ in hcs])], local_sem=S.sent)
    sent += E_ON
    g.wait_ge(S.wdl, 32)
    for r, (a, dst) in enumerate(relays[me]):
        _write(g, T, topo, core, a, T.wd[:], T.wd[:], arr(me), _take([stay, other][r % 2], E_ON))
        sent += E_ON
    for p, k in enumerate(direct[me]):
        t = tgt(me, k)
        _write(g, T, topo, core, t, _blk(T, me), T.wd[:], arr(me), _take(topo.mask(core, t), E_OFF))
        sent += E_OFF
        if p == 0:
            g.wait_ge(S.xl, 16)
            g.wait_ge(S.dl, 16)
            _write(g, T, topo, core, hcs[0], T.xd[:], T.xd[:], S.xa, _take(stay, E_ON))
            sent += E_ON
    _write(g, T, topo, core, hcs[1], T.xd[:], T.xd[:], S.xa, _take(other, E_ON))
    sent += E_ON
    g.wait_ge(S.sent, sent)

    arrive = {j: (arr(j), E_OFF) for _, j in order[me]}
    arrive[me] = (S.wl, 32)
    _pipeline(g, T, order[me], arrive, (S.xl, 16), (S.dl, 16), (S.idr, 1), [(ap, sem, E_ON) for ap, sem in halves(0)])

    hv = halves(1)
    for h, (acc, dd, ev) in enumerate([(T.acc0, S.dd0, S.ev0), (T.acc1, S.dd1, S.ev1)]):
        g.vector.wait_ge(dd, 1)
        g.vector.wait_ge(hv[h][1], E_ON)
        g.vector.tensor_tensor(T.outb[:, h * HF:(h + 1) * HF], acc[:, 0:HF], hv[h][0], AluOpType.add).then_inc(ev, 1)
    g.scalar.wait_ge(S.ev0, 1)
    g.scalar.dma_start(T.dx[:, 0:HF], T.outb[:, 0:HF]).then_inc(S.st0, 16)
    g.scalar.wait_ge(S.st0, 16)
    g.sync.wait_ge(S.ev1, 1)
    g.sync.dma_start(T.dx[:, HF:TK], T.outb[:, HF:TK]).then_inc(S.st1, 16)
    g.sync.wait_ge(S.st1, 16)
